import numpy as np
import ml_dtypes


def mxq(x, axis, fmt="e4m3"):
    dtype, down = {"e4m3": (ml_dtypes.float8_e4m3fn, 7), "e5m2": (ml_dtypes.float8_e5m2, 14)}[fmt]
    v = np.moveaxis(np.asarray(x, np.float32).astype(ml_dtypes.bfloat16).astype(np.float64), axis, -1)
    blocks = v.reshape(v.shape[:-1] + (-1, 32))
    amax = np.abs(blocks).max(-1, keepdims=True)
    byte = np.maximum(np.where(amax > 0, np.frexp(amax)[1] - 1 + 127, 0) - down, 1)
    scale = np.exp2(byte - 127.0)
    codes = (blocks / scale).astype(np.float32).astype(dtype).astype(np.float64)
    return np.moveaxis((codes * scale).reshape(v.shape), -1, axis)


WIDE = False


def mx_kscale(k):
    if not WIDE:
        return np.ones(k)
    levels = np.array([30, -30])
    if k % 512:
        return np.exp2(np.random.permutation(np.resize(levels, k // 32))).repeat(32)
    a = np.empty((k // 512, 16))
    for p in range(k // 512):
        a[p, :8] = np.random.permutation(np.resize(levels, 8))
        for g in range(8):
            far = levels[np.abs(levels - a[p, g]) >= 10]
            a[p, g + 8] = far[np.random.randint(len(far))]
    return np.exp2(a.ravel()).repeat(32)


def f64(x):
    return np.asarray(x).astype(np.float64)


def striped(idx):
    return np.tile(np.asarray(idx).reshape(-1, 16).T, (8, 1)).astype(np.uint16)


def unstriped(offs):
    return offs[:16].T.reshape(-1).astype(np.int64)


E2M1 = np.array([0.0, 0.5, 1.0, 1.5, 2.0, 3.0, 4.0, 6.0, -0.0, -0.5, -1.0, -1.5, -2.0, -3.0, -4.0, -6.0])


def pack_weight(w, fmt):
    k, n = w.shape
    w = f64(np.asarray(w, np.float32).astype(ml_dtypes.bfloat16)).reshape(k // 32, 32, n)
    amax = np.abs(w).max(1)
    if fmt == "e4m3":
        byte = np.frexp(amax)[1] - 1 + 127 - 7
    else:
        mant, ex = np.frexp(amax / 6.0)
        byte = np.where(mant > 0.5, ex, ex - 1) + 127
    byte = np.clip(np.where(amax > 0, byte, 1), 1, 254)
    scaled = (w * np.exp2(127.0 - byte)[:, None, :]).reshape(k, n).astype(np.float32)
    by_word = np.ascontiguousarray(scaled.reshape(k // 512, 128, 4, n).transpose(0, 1, 3, 2))
    if fmt == "e4m3":
        words = by_word.astype(ml_dtypes.float8_e4m3fn).view(np.uint8)
    else:
        c = by_word.astype(ml_dtypes.float4_e2m1fn).view(np.uint8) & 0xF
        words = (c[..., 0::2] | (c[..., 1::2] << 4)).reshape(k // 512, 128, 2 * n)
    return np.ascontiguousarray(words), np.ascontiguousarray(byte.astype(np.uint8).reshape(k // 512, 16, n))


def unpack_weight(words, scales, fmt):
    g, _, n = scales.shape
    words = np.ascontiguousarray(words).reshape(g, 128, n, -1)
    if fmt == "e4m3":
        vals = words.view(ml_dtypes.float8_e4m3fn).astype(np.float64)
    else:
        nib = np.empty((g, 128, n, 4), np.uint8)
        nib[..., 0::2] = words & 0xF
        nib[..., 1::2] = words >> 4
        vals = E2M1[nib]
    vals = vals * np.repeat(np.exp2(scales.astype(np.float64) - 127.0), 8, axis=1)[..., None]
    return vals.transpose(0, 1, 3, 2).reshape(g * 512, n)


def sigmoid(v):
    return 1.0 / (1.0 + np.exp(-v))


K, F, T, Z, J, R, C, Q, O, N, E = 512, 512, 1024, 1024, 256, 512, 512, 1024, 256, 256, 1024


def setup_inputs():
    n = np.random.standard_normal
    idx = np.random.permutation(T)[:J]
    idx2 = np.random.permutation(Z)[:J]
    idx3 = np.random.permutation(C)[:J]
    idx4 = np.random.permutation(Q)[:C]
    idx5 = np.random.permutation(C)[:O]
    idx6 = np.random.permutation(E)[:O]
    fk = mx_kscale(K)
    fr = mx_kscale(R)
    ff = mx_kscale(F)
    xtp = pack_weight(n((K, T)) / fk[:, None], "e2m1")
    wp = pack_weight(n((K, R)) * 1 / np.sqrt(K) * fk[:, None] * fr, "e4m3")
    xop = pack_weight(n((F, Z)) / ff[:, None], "e4m3")
    w0p = pack_weight(n((F, R)) * 1 / np.sqrt(F) * ff[:, None] * fr, "e2m1")
    wbp = pack_weight(n((R, N)) * 1 / np.sqrt(R) / fr[:, None], "e2m1")
    return {
        "xt_words": xtp[0],
        "xt_scales": xtp[1],
        "w_words": wp[0],
        "w_scales": wp[1],
        "xo_words": xop[0],
        "xo_scales": xop[1],
        "w0_words": w0p[0],
        "w0_scales": w0p[1],
        "tg": (1.0 * n((R, Q))).astype(np.float32),
        "sg": (np.random.uniform(0.6, 1.6, (R, 1))).astype(np.float32),
        "bg": (np.random.uniform(-1.0, 1.0, (R, 1))).astype(np.float32),
        "wb_words": wbp[0],
        "wb_scales": wbp[1],
        "offs": striped(idx),
        "offs2": striped(idx2),
        "offs3": striped(idx3),
        "offs4": striped(idx4),
        "offs5": striped(idx5),
        "offs6": striped(idx6),
    }


def reference(xt_words, xt_scales, w_words, w_scales, xo_words, xo_scales, w0_words, w0_scales, tg, sg, bg, wb_words, wb_scales, offs, offs2, offs3, offs4, offs5, offs6):
    idx = unstriped(offs)
    idx2 = unstriped(offs2)
    idx3 = unstriped(offs3)
    idx4 = unstriped(offs4)
    idx5 = unstriped(offs5)
    idx6 = unstriped(offs6)
    xtu = unpack_weight(xt_words, xt_scales, "e2m1")
    wu = unpack_weight(w_words, w_scales, "e4m3")
    xou = unpack_weight(xo_words, xo_scales, "e4m3")
    w0u = unpack_weight(w0_words, w0_scales, "e2m1")
    wbu = unpack_weight(wb_words, wb_scales, "e2m1")
    xtidxg = xtu[:, idx]
    xoidx2g = xou[:, idx2]
    a = wu.T @ xtidxg + w0u.T @ xoidx2g
    pw = np.zeros((R, C))
    pw[:, idx3] = a
    pg = pw * sigmoid(f64(tg)[:, idx4] * f64(sg) + f64(bg))
    hid = pg[:, idx5]
    hidq = mxq(hid, 0, "e5m2")
    p = wbu.T @ hidq
    y = np.zeros((N, E))
    y[:, idx6] = p
    return y

@@ -1,0 +1,177 @@
+from contextlib import ExitStack
+
+import concourse.mybir as mybir
+
+F32 = mybir.dt.float32
+BF16 = mybir.dt.bfloat16
+I32 = mybir.dt.int32
+U32 = mybir.dt.uint32
+U16 = mybir.dt.uint16
+U8 = mybir.dt.uint8
+E4M3 = mybir.dt.float8_e4m3fn_x4
+E5M2 = mybir.dt.float8_e5m2_x4
+E2M1 = mybir.dt.float4_e2m1fn_x4
+ACT = mybir.ActivationFunctionType
+MULT = mybir.AluOpType.mult
+
+P = 128
+PACK = 4
+T, Z, J, R, C, Q, O, N, E = 1024, 1024, 256, 512, 512, 1024, 256, 256, 1024
+FLOPS = 2 * 512 * R * J * 2 + 2 * R * N * O
+
+
+def load_scales(queue, plane, scales, quads=range(4)):
+    for quad in quads:
+        queue.dma_start(
+            out=plane[32 * quad : 32 * quad + 4, :].bitcast(I32),
+            in_=scales[0, 4 * quad : 4 * quad + 4, :].bitcast(I32),
+        )
+
+
+def tile_list_gatedpage_bank_one_scattered_kernel(
+    tc, xt_words, xt_scales, w_words, w_scales, xo_words, xo_scales, w0_words, w0_scales,
+    tg, sg, bg, wb_words, wb_scales, offs, offs2, offs3, offs4, offs5, offs6, out,
+):
+    nc = tc.nc
+    with ExitStack() as ctx:
+        keep = ctx.enter_context(tc.tile_pool(name="keep", bufs=1))
+        psum = ctx.enter_context(tc.psum_pool(name="psum", bufs=1))
+
+        def sb(shape, dtype, name):
+            return keep.tile(shape, dtype, name=name, align_bytes=64)
+
+        l1 = keep.tile([P, J // 16], U16, name="l1")
+        l2 = keep.tile([P, J // 16], U16, name="l2")
+        l3 = keep.tile([P, J // 16], U16, name="l3")
+        l4 = keep.tile([P, C // 16], U16, name="l4")
+        l5 = keep.tile([P, O // 16], U16, name="l5")
+        l6 = keep.tile([P, O // 16], U16, name="l6")
+
+        xt_w = sb([P, T], U16, "xt_w")
+        xt_s = sb([P, T], U8, "xt_s")
+        xo_w = sb([P, Z], U32, "xo_w")
+        xo_s = sb([P, Z], U8, "xo_s")
+        w_w = sb([P, R], U32, "w_w")
+        w0_w = sb([P, R], U16, "w0_w")
+        w_s = sb([P, R], U8, "w_s")
+        w0_s = sb([P, R], U8, "w0_s")
+        wb_w = sb([P, N], U16, "wb_w")
+        wb_s = sb([P, N], U8, "wb_s")
+        slope = sb([P, PACK], F32, "slope")
+        offset = sb([P, PACK], F32, "offset")
+        table = [sb([P, Q], F32, "table%d" % t) for t in range(PACK)]
+        board = [sb([P, C], F32, "board%d" % t) for t in range(PACK)]
+        page = [sb([P, E], F32, "page%d" % h) for h in range(2)]
+
+        for plane in (xt_s, w_s, w0_s, xo_s, wb_s):
+            nc.vector.memset(plane[:].bitcast(I32), 0)
+        for t in range(PACK):
+            nc.vector.memset(board[t][:], 0.0)
+
+        tg_rows = tg.rearrange("(p t) q -> t p q", t=PACK)
+        nc.gpsimd.dma_start(out=slope[:], in_=sg.rearrange("(p t) o -> p (t o)", t=PACK))
+        nc.gpsimd.dma_start(out=offset[:], in_=bg.rearrange("(p t) o -> p (t o)", t=PACK))
+        nc.sync.dma_start(l1[:], offs)
+        nc.sync.dma_start(out=xt_w[:].bitcast(I32), in_=xt_words[0].bitcast(I32))
+        nc.sync.dma_start(out=w_w[:].bitcast(I32), in_=w_words[0].rearrange("p n t -> p (n t)").bitcast(I32))
+        nc.sync.dma_start(out=xo_w[:].bitcast(I32), in_=xo_words[0].rearrange("p n t -> p (n t)").bitcast(I32))
+        load_scales(nc.sync, xt_s, xt_scales)
+        load_scales(nc.sync, w_s, w_scales)
+        nc.sync.dma_start(l2[:], offs2)
+        nc.sync.dma_start(out=w0_w[:].bitcast(I32), in_=w0_words[0].bitcast(I32))
+        nc.sync.dma_start(l4[:], offs4)
+        nc.sync.dma_start(out=table[0][:], in_=tg_rows[0])
+        load_scales(nc.gpsimd, w0_s, w0_scales, range(1))
+        load_scales(nc.sync, xo_s, xo_scales)
+        load_scales(nc.sync, w0_s, w0_scales, range(1, 4))
+        nc.sync.dma_start(out=table[1][:], in_=tg_rows[1])
+        nc.sync.dma_start(l3[:], offs3)
+        for t in range(2, PACK):
+            nc.sync.dma_start(out=table[t][:], in_=tg_rows[t])
+        nc.sync.dma_start(l5[:], offs5)
+        nc.sync.dma_start(l6[:], offs6)
+        nc.gpsimd.dma_start(out=wb_w[:].bitcast(I32), in_=wb_words[0].bitcast(I32))
+        load_scales(nc.gpsimd, wb_s, wb_scales)
+        for h in range(2):
+            nc.gpsimd.memset(page[h][:], 0.0)
+
+        tok_w = sb([P, J], U16, "tok_w")
+        tok_s = sb([P, J], U8, "tok_s")
+        note_w = sb([P, J], U32, "note_w")
+        note_s = sb([P, J], U8, "note_s")
+        wp_w = sb([P, R], U32, "wp_w")
+        wp_s = sb([P, R], U8, "wp_s")
+        w0p_w = sb([P, R], U16, "w0p_w")
+        w0p_s = sb([P, R], U8, "w0p_s")
+
+        def deal(dealt, natural):
+            nc.vector.tensor_copy(out=dealt[:].rearrange("p (t m) -> p t m", t=PACK),
+                                  in_=natural[:].rearrange("p (m t) -> p t m", t=PACK))
+
+        nc.vector.tensor_copy(tok_w[:], xt_w[:].indirect(l1[:]))
+        deal(wp_w, w_w)
+        nc.vector.tensor_copy(tok_s[:], xt_s[:].indirect(l1[:]))
+        deal(wp_s, w_s)
+        nc.vector.tensor_copy(note_w[:], xo_w[:].indirect(l2[:]))
+        deal(w0p_w, w0_w)
+        nc.vector.tensor_copy(note_s[:], xo_s[:].indirect(l2[:]))
+        deal(w0p_s, w0_s)
+
+        acc = [psum.tile([P, 512], F32, name="acc%d" % t) for t in range(PACK)]
+        for t in range(PACK):
+            cols = slice(P * t, P * (t + 1))
+            nc.tensor.matmul_mx(out=acc[t][:, 0:J], lhsT=wp_w[:, cols].bitcast(E4M3), lhsT_scale=wp_s[:, cols],
+                                rhs=tok_w[:].bitcast(E2M1), rhs_scale=tok_s[:], start=True, stop=False)
+        for t in range(PACK):
+            cols = slice(P * t, P * (t + 1))
+            nc.tensor.matmul_mx(out=acc[t][:, 0:J], lhsT=w0p_w[:, cols].bitcast(E2M1), lhsT_scale=w0p_s[:, cols],
+                                rhs=note_w[:].bitcast(E4M3), rhs_scale=note_s[:], start=False, stop=True)
+
+        gate = [sb([P, C], F32, "gate%d" % t) for t in range(PACK)]
+        slots = [sb([P, J], F32, "slots%d" % t) for t in range(PACK)]
+        gated = [sb([P, C], F32, "gated%d" % t) for t in range(PACK)]
+        hid = sb([P, O, PACK], BF16, "hid")
+        picked = sb([P, 2, O], BF16, "picked")
+
+        def look_up_gate(t):
+            nc.scalar.activation(out=gate[t][:], in_=table[t][:].indirect(l4[:]), func=ACT.Sigmoid,
+                                 bias=offset[:, t : t + 1], scale=slope[:, t : t + 1])
+
+        def place_on_scalar(t):
+            nc.scalar.copy(out=slots[t][:], in_=acc[t][:, 0:J])
+            nc.scalar.activation(out=board[t][:].indirect(l3[:]), in_=slots[t][:], func=ACT.Copy)
+
+        for t in range(3):
+            look_up_gate(t)
+        for t in range(2):
+            nc.vector.tensor_copy(out=slots[t][:], in_=acc[t][:, 0:J])
+        for t in range(2):
+            nc.vector.tensor_copy(board[t][:].indirect(l3[:]), slots[t][:])
+        place_on_scalar(2)
+        look_up_gate(3)
+        place_on_scalar(3)
+        for t in range(3):
+            nc.vector.tensor_tensor(gated[t][:], board[t][:], gate[t][:], MULT)
+        for t in range(2):
+            nc.scalar.activation(out=picked[:, t, :], in_=gated[t][:].indirect(l5[:]), func=ACT.Copy)
+        nc.vector.tensor_copy(hid[:, :, 2], gated[2][:].indirect(l5[:]))
+        nc.vector.tensor_tensor(gated[3][:], board[3][:], gate[3][:], MULT)
+        nc.vector.tensor_copy(hid[:, :, 3], gated[3][:].indirect(l5[:]))
+        nc.vector.tensor_copy(out=hid[:, :, 0:2], in_=picked[:].rearrange("p t o -> p o t"))
+
+        hid_w = sb([P, O], U32, "hid_w")
+        hid_s = sb([P, O], U8, "hid_s")
+        nc.vector.quantize_mx(out=hid_w[:].bitcast(E5M2), scales=hid_s[:], in_=hid[:].rearrange("p o t -> p (o t)"))
+
+        res = [psum.tile([P, 512], F32, name="res%d" % h) for h in range(2)]
+        rows = [sb([P, O], F32, "rows%d" % h) for h in range(2)]
+        for h in range(2):
+            cols = slice(P * h, P * (h + 1))
+            nc.tensor.matmul_mx(out=res[h][:, 0:O], lhsT=wb_w[:, cols].bitcast(E2M1), lhsT_scale=wb_s[:, cols],
+                                rhs=hid_w[:].bitcast(E5M2), rhs_scale=hid_s[:], start=True, stop=True)
+        nc.scalar.copy(out=rows[0][:], in_=res[0][:, 0:O])
+        nc.scalar.activation(out=page[0][:].indirect(l6[:]), in_=rows[0][:], func=ACT.Copy)
+        nc.vector.tensor_copy(out=rows[1][:], in_=res[1][:, 0:O])
+        nc.vector.tensor_copy(page[1][:].indirect(l6[:]), rows[1][:])
+        nc.scalar.dma_start(out=out[0:P, :], in_=page[0][:])
+        nc.sync.dma_start(out=out[P : 2 * P, :], in_=page[1][:])

@@ -20,14 +20,6 @@ T, Z, J, R, C, Q, O, N, E = 1024, 1024, 256, 512, 512, 1024, 256, 256, 1024
 FLOPS = 2 * 512 * R * J * 2 + 2 * R * N * O
 
 
-def load_scales(queue, plane, scales, quads=range(4)):
-    for quad in quads:
-        queue.dma_start(
-            out=plane[32 * quad : 32 * quad + 4, :].bitcast(I32),
-            in_=scales[0, 4 * quad : 4 * quad + 4, :].bitcast(I32),
-        )
-
-
 def tile_list_gatedpage_bank_one_scattered_kernel(
     tc, xt_words, xt_scales, w_words, w_scales, xo_words, xo_scales, w0_words, w0_scales,
     tg, sg, bg, wb_words, wb_scales, offs, offs2, offs3, offs4, offs5, offs6, out,
@@ -49,115 +41,115 @@ def tile_list_gatedpage_bank_one_scattered_kernel(
 
         xt_w = sb([P, T], U16, "xt_w")
         xt_s = sb([P, T], U8, "xt_s")
-        xo_w = sb([P, Z], U32, "xo_w")
+        xo_w = keep.tile([P, Z], U32, name="xo_w", tag="wide3")
         xo_s = sb([P, Z], U8, "xo_s")
         w_w = sb([P, R], U32, "w_w")
         w0_w = sb([P, R], U16, "w0_w")
-        w_s = sb([P, R], U8, "w_s")
-        w0_s = sb([P, R], U8, "w0_s")
-        wb_w = sb([P, N], U16, "wb_w")
-        wb_s = sb([P, N], U8, "wb_s")
+        ww_s = sb([P, 2 * R], U8, "ww_s")
+        planes = sb([P, 2 * R + 2 * J + N], U8, "planes")
+        wb_s = planes[:, 2 * R + 2 * J : 2 * R + 2 * J + N]
         slope = sb([P, PACK], F32, "slope")
         offset = sb([P, PACK], F32, "offset")
-        table = [sb([P, Q], F32, "table%d" % t) for t in range(PACK)]
+        table = [keep.tile([P, Q], F32, name="table%d" % t, tag="wide%d" % t) for t in range(2)]
         board = [sb([P, C], F32, "board%d" % t) for t in range(PACK)]
-        page = [sb([P, E], F32, "page%d" % h) for h in range(2)]
 
-        for plane in (xt_s, w_s, w0_s, xo_s, wb_s):
-            nc.vector.memset(plane[:].bitcast(I32), 0)
+        for plane in (xt_s[:], xo_s[:], ww_s[:], wb_s):
+            nc.vector.memset(plane.bitcast(I32), 0)
         for t in range(PACK):
             nc.vector.memset(board[t][:], 0.0)
 
         tg_rows = tg.rearrange("(p t) q -> t p q", t=PACK)
-        nc.gpsimd.dma_start(out=slope[:], in_=sg.rearrange("(p t) o -> p (t o)", t=PACK))
-        nc.gpsimd.dma_start(out=offset[:], in_=bg.rearrange("(p t) o -> p (t o)", t=PACK))
+        for t in range(2):
+            nc.gpsimd.dma_start(out=table[t][:], in_=tg_rows[t])
+        wb_w = sb([P, N], U16, "wb_w")
         nc.sync.dma_start(l1[:], offs)
-        nc.sync.dma_start(out=xt_w[:].bitcast(I32), in_=xt_words[0].bitcast(I32))
-        nc.sync.dma_start(out=w_w[:].bitcast(I32), in_=w_words[0].rearrange("p n t -> p (n t)").bitcast(I32))
-        nc.sync.dma_start(out=xo_w[:].bitcast(I32), in_=xo_words[0].rearrange("p n t -> p (n t)").bitcast(I32))
-        load_scales(nc.sync, xt_s, xt_scales)
-        load_scales(nc.sync, w_s, w_scales)
         nc.sync.dma_start(l2[:], offs2)
-        nc.sync.dma_start(out=w0_w[:].bitcast(I32), in_=w0_words[0].bitcast(I32))
         nc.sync.dma_start(l4[:], offs4)
-        nc.sync.dma_start(out=table[0][:], in_=tg_rows[0])
-        load_scales(nc.gpsimd, w0_s, w0_scales, range(1))
-        load_scales(nc.sync, xo_s, xo_scales)
-        load_scales(nc.sync, w0_s, w0_scales, range(1, 4))
-        nc.sync.dma_start(out=table[1][:], in_=tg_rows[1])
+        nc.sync.dma_start(out=slope[:], in_=sg.rearrange("(p t) o -> p (t o)", t=PACK))
+        nc.sync.dma_start(out=offset[:], in_=bg.rearrange("(p t) o -> p (t o)", t=PACK))
+        nc.sync.dma_start(out=xt_s[0:16, :].bitcast(I32), in_=xt_scales[0].bitcast(I32))
+        nc.sync.dma_start(out=xo_s[0:16, :].bitcast(I32), in_=xo_scales[0].bitcast(I32))
+        nc.sync.dma_start(out=xo_w[:].bitcast(I32), in_=xo_words[0].rearrange("p n t -> p (n t)").bitcast(I32))
+        nc.sync.dma_start(out=ww_s[0:16, 0:R].bitcast(I32), in_=w_scales[0].bitcast(I32))
+        nc.sync.dma_start(out=ww_s[0:16, R : 2 * R].bitcast(I32), in_=w0_scales[0].bitcast(I32))
+        nc.sync.dma_start(out=wb_s[0:16, :].bitcast(I32), in_=wb_scales[0].bitcast(I32))
+        nc.sync.dma_start(out=xt_w[:].bitcast(I32), in_=xt_words[0].bitcast(I32))
         nc.sync.dma_start(l3[:], offs3)
-        for t in range(2, PACK):
-            nc.sync.dma_start(out=table[t][:], in_=tg_rows[t])
+        nc.sync.dma_start(out=w_w[:].bitcast(I32), in_=w_words[0].rearrange("p n t -> p (n t)").bitcast(I32))
+        nc.sync.dma_start(out=w0_w[:].bitcast(I32), in_=w0_words[0].bitcast(I32))
         nc.sync.dma_start(l5[:], offs5)
         nc.sync.dma_start(l6[:], offs6)
-        nc.gpsimd.dma_start(out=wb_w[:].bitcast(I32), in_=wb_words[0].bitcast(I32))
-        load_scales(nc.gpsimd, wb_s, wb_scales)
-        for h in range(2):
-            nc.gpsimd.memset(page[h][:], 0.0)
+        nc.sync.dma_start(out=wb_w[:].bitcast(I32), in_=wb_words[0].bitcast(I32))
 
         tok_w = sb([P, J], U16, "tok_w")
         tok_s = sb([P, J], U8, "tok_s")
         note_w = sb([P, J], U32, "note_w")
-        note_s = sb([P, J], U8, "note_s")
+        note_s = keep.tile([P, J], U8, name="note_s", tag="wide2")
         wp_w = sb([P, R], U32, "wp_w")
-        wp_s = sb([P, R], U8, "wp_s")
         w0p_w = sb([P, R], U16, "w0p_w")
-        w0p_s = sb([P, R], U8, "w0p_s")
 
         def deal(dealt, natural):
-            nc.vector.tensor_copy(out=dealt[:].rearrange("p (t m) -> p t m", t=PACK),
-                                  in_=natural[:].rearrange("p (m t) -> p t m", t=PACK))
+            nc.vector.tensor_copy(out=dealt[:].rearrange("p (t m) -> p m t", t=PACK),
+                                  in_=natural[:].rearrange("p (m t) -> p m t", t=PACK))
 
+        nc.vector.tensor_copy(tok_s[:], xt_s[:].indirect(l1[:]))
+        nc.vector.tensor_copy(note_s[:], xo_s[:].indirect(l2[:]))
+        nc.vector.tensor_copy(out=planes[:, 2 * R : 2 * R + J].bitcast(I32), in_=tok_s[:].bitcast(I32))
+        nc.vector.tensor_copy(out=planes[:, 0 : 2 * R].rearrange("p (w t m) -> p w m t", w=2, t=PACK),
+                              in_=ww_s[:].rearrange("p (w m t) -> p w m t", w=2, t=PACK))
+        nc.vector.tensor_copy(out=planes[:, 2 * R + J : 2 * R + 2 * J].bitcast(I32), in_=note_s[:].bitcast(I32))
+        for quad in range(1, 4):
+            nc.sync.dma_start(out=planes[32 * quad : 32 * quad + 4, :].bitcast(I32),
+                              in_=planes[4 * quad : 4 * quad + 4, :].bitcast(I32))
+        nc.vector.tensor_copy(note_w[:], xo_w[:].indirect(l2[:]))
+        for t in range(2, PACK):
+            table.append(keep.tile([P, Q], F32, name="table%d" % t, tag="wide%d" % t))
+            nc.sync.dma_start(out=table[t][:], in_=tg_rows[t])
         nc.vector.tensor_copy(tok_w[:], xt_w[:].indirect(l1[:]))
         deal(wp_w, w_w)
-        nc.vector.tensor_copy(tok_s[:], xt_s[:].indirect(l1[:]))
-        deal(wp_s, w_s)
-        nc.vector.tensor_copy(note_w[:], xo_w[:].indirect(l2[:]))
         deal(w0p_w, w0_w)
-        nc.vector.tensor_copy(note_s[:], xo_s[:].indirect(l2[:]))
-        deal(w0p_s, w0_s)
+        wp_s = planes[:, 0:R]
+        w0p_s = planes[:, R : 2 * R]
+        tok_p = planes[:, 2 * R : 2 * R + J]
+        note_p = planes[:, 2 * R + J : 2 * R + 2 * J]
 
         acc = [psum.tile([P, 512], F32, name="acc%d" % t) for t in range(PACK)]
         for t in range(PACK):
             cols = slice(P * t, P * (t + 1))
             nc.tensor.matmul_mx(out=acc[t][:, 0:J], lhsT=wp_w[:, cols].bitcast(E4M3), lhsT_scale=wp_s[:, cols],
-                                rhs=tok_w[:].bitcast(E2M1), rhs_scale=tok_s[:], start=True, stop=False)
-        for t in range(PACK):
-            cols = slice(P * t, P * (t + 1))
+                                rhs=tok_w[:].bitcast(E2M1), rhs_scale=tok_p, start=True, stop=False)
             nc.tensor.matmul_mx(out=acc[t][:, 0:J], lhsT=w0p_w[:, cols].bitcast(E2M1), lhsT_scale=w0p_s[:, cols],
-                                rhs=note_w[:].bitcast(E4M3), rhs_scale=note_s[:], start=False, stop=True)
+                                rhs=note_w[:].bitcast(E4M3), rhs_scale=note_p, start=False, stop=True)
 
         gate = [sb([P, C], F32, "gate%d" % t) for t in range(PACK)]
         slots = [sb([P, J], F32, "slots%d" % t) for t in range(PACK)]
         gated = [sb([P, C], F32, "gated%d" % t) for t in range(PACK)]
         hid = sb([P, O, PACK], BF16, "hid")
-        picked = sb([P, 2, O], BF16, "picked")
+        picked = sb([P, PACK, O], BF16, "picked")
 
         def look_up_gate(t):
             nc.scalar.activation(out=gate[t][:], in_=table[t][:].indirect(l4[:]), func=ACT.Sigmoid,
                                  bias=offset[:, t : t + 1], scale=slope[:, t : t + 1])
 
-        def place_on_scalar(t):
-            nc.scalar.copy(out=slots[t][:], in_=acc[t][:, 0:J])
-            nc.scalar.activation(out=board[t][:].indirect(l3[:]), in_=slots[t][:], func=ACT.Copy)
-
         for t in range(3):
             look_up_gate(t)
-        for t in range(2):
+        for t in (0, 2):
             nc.vector.tensor_copy(out=slots[t][:], in_=acc[t][:, 0:J])
-        for t in range(2):
             nc.vector.tensor_copy(board[t][:].indirect(l3[:]), slots[t][:])
-        place_on_scalar(2)
+        nc.scalar.copy(out=slots[1][:], in_=acc[1][:, 0:J])
         look_up_gate(3)
-        place_on_scalar(3)
-        for t in range(3):
+        nc.scalar.copy(out=slots[3][:], in_=acc[3][:, 0:J])
+        for t in (1, 3):
+            nc.scalar.activation(out=board[t][:].indirect(l3[:]), in_=slots[t][:], func=ACT.Copy)
+        for t in range(PACK):
             nc.vector.tensor_tensor(gated[t][:], board[t][:], gate[t][:], MULT)
-        for t in range(2):
+        for t in range(3):
             nc.scalar.activation(out=picked[:, t, :], in_=gated[t][:].indirect(l5[:]), func=ACT.Copy)
-        nc.vector.tensor_copy(hid[:, :, 2], gated[2][:].indirect(l5[:]))
-        nc.vector.tensor_tensor(gated[3][:], board[3][:], gate[3][:], MULT)
-        nc.vector.tensor_copy(hid[:, :, 3], gated[3][:].indirect(l5[:]))
-        nc.vector.tensor_copy(out=hid[:, :, 0:2], in_=picked[:].rearrange("p t o -> p o t"))
+        nc.vector.tensor_copy(picked[:, 3, :], gated[3][:].indirect(l5[:]))
+        nc.vector.tensor_copy(out=hid[:], in_=picked[:].rearrange("p t o -> p o t"))
+        page = [keep.tile([P, E], F32, name="page%d" % h, tag="wide%d" % (h + 2)) for h in range(2)]
+        for h in range(2):
+            nc.gpsimd.memset(page[h][:], 0.0)
 
         hid_w = sb([P, O], U32, "hid_w")
         hid_s = sb([P, O], U8, "hid_s")

@@ -16,8 +16,15 @@ MULT = mybir.AluOpType.mult
 
 P = 128
 PACK = 4
+K_PASS = P * PACK
+SCALE_ROWS = K_PASS // 32
+QUADRANT = 32
+QUAD_ROWS = 4
+BANK = 512
+LIST_ROWS = 16
 T, Z, J, R, C, Q, O, N, E = 1024, 1024, 256, 512, 512, 1024, 256, 256, 1024
-FLOPS = 2 * 512 * R * J * 2 + 2 * R * N * O
+EARLY_TABLES = 2
+FLOPS = 2 * K_PASS * R * J * 2 + 2 * R * N * O
 
 
 def tile_list_gatedpage_bank_one_scattered_kernel(
@@ -32,12 +39,12 @@ def tile_list_gatedpage_bank_one_scattered_kernel(
         def sb(shape, dtype, name):
             return keep.tile(shape, dtype, name=name, align_bytes=64)
 
-        l1 = keep.tile([P, J // 16], U16, name="l1")
-        l2 = keep.tile([P, J // 16], U16, name="l2")
-        l3 = keep.tile([P, J // 16], U16, name="l3")
-        l4 = keep.tile([P, C // 16], U16, name="l4")
-        l5 = keep.tile([P, O // 16], U16, name="l5")
-        l6 = keep.tile([P, O // 16], U16, name="l6")
+        l1 = keep.tile([P, J // LIST_ROWS], U16, name="l1")
+        l2 = keep.tile([P, J // LIST_ROWS], U16, name="l2")
+        l3 = keep.tile([P, J // LIST_ROWS], U16, name="l3")
+        l4 = keep.tile([P, C // LIST_ROWS], U16, name="l4")
+        l5 = keep.tile([P, O // LIST_ROWS], U16, name="l5")
+        l6 = keep.tile([P, O // LIST_ROWS], U16, name="l6")
 
         xt_w = sb([P, T], U16, "xt_w")
         xt_s = sb([P, T], U8, "xt_s")
@@ -48,18 +55,18 @@ def tile_list_gatedpage_bank_one_scattered_kernel(
         ww_s = sb([P, 2 * R], U8, "ww_s")
         planes = sb([P, 2 * R + 2 * J + N], U8, "planes")
         wb_s = planes[:, 2 * R + 2 * J : 2 * R + 2 * J + N]
-        slope = sb([P, PACK], F32, "slope")
+        slope = keep.tile([P, PACK], F32, name="slope", tag="picked")
         offset = sb([P, PACK], F32, "offset")
-        table = [keep.tile([P, Q], F32, name="table%d" % t, tag="wide%d" % t) for t in range(2)]
+        table = [keep.tile([P, Q], F32, name="table%d" % t, tag="wide%d" % t) for t in range(EARLY_TABLES)]
         board = [sb([P, C], F32, "board%d" % t) for t in range(PACK)]
 
-        for plane in (xt_s[:], xo_s[:], ww_s[:], wb_s):
-            nc.vector.memset(plane.bitcast(I32), 0)
+        for scale_bytes in (xt_s[:], xo_s[:], ww_s[:], wb_s):
+            nc.vector.memset(scale_bytes.bitcast(I32), 0)
         for t in range(PACK):
             nc.vector.memset(board[t][:], 0.0)
 
         tg_rows = tg.rearrange("(p t) q -> t p q", t=PACK)
-        for t in range(2):
+        for t in range(EARLY_TABLES):
             nc.gpsimd.dma_start(out=table[t][:], in_=tg_rows[t])
         wb_w = sb([P, N], U16, "wb_w")
         nc.sync.dma_start(l1[:], offs)
@@ -67,12 +74,12 @@ def tile_list_gatedpage_bank_one_scattered_kernel(
         nc.sync.dma_start(l4[:], offs4)
         nc.sync.dma_start(out=slope[:], in_=sg.rearrange("(p t) o -> p (t o)", t=PACK))
         nc.sync.dma_start(out=offset[:], in_=bg.rearrange("(p t) o -> p (t o)", t=PACK))
-        nc.sync.dma_start(out=xt_s[0:16, :].bitcast(I32), in_=xt_scales[0].bitcast(I32))
-        nc.sync.dma_start(out=xo_s[0:16, :].bitcast(I32), in_=xo_scales[0].bitcast(I32))
+        nc.sync.dma_start(out=xt_s[0:SCALE_ROWS, :].bitcast(I32), in_=xt_scales[0].bitcast(I32))
+        nc.sync.dma_start(out=xo_s[0:SCALE_ROWS, :].bitcast(I32), in_=xo_scales[0].bitcast(I32))
         nc.sync.dma_start(out=xo_w[:].bitcast(I32), in_=xo_words[0].rearrange("p n t -> p (n t)").bitcast(I32))
-        nc.sync.dma_start(out=ww_s[0:16, 0:R].bitcast(I32), in_=w_scales[0].bitcast(I32))
-        nc.sync.dma_start(out=ww_s[0:16, R : 2 * R].bitcast(I32), in_=w0_scales[0].bitcast(I32))
-        nc.sync.dma_start(out=wb_s[0:16, :].bitcast(I32), in_=wb_scales[0].bitcast(I32))
+        nc.sync.dma_start(out=ww_s[0:SCALE_ROWS, 0:R].bitcast(I32), in_=w_scales[0].bitcast(I32))
+        nc.sync.dma_start(out=ww_s[0:SCALE_ROWS, R : 2 * R].bitcast(I32), in_=w0_scales[0].bitcast(I32))
+        nc.sync.dma_start(out=wb_s[0:SCALE_ROWS, :].bitcast(I32), in_=wb_scales[0].bitcast(I32))
         nc.sync.dma_start(out=xt_w[:].bitcast(I32), in_=xt_words[0].bitcast(I32))
         nc.sync.dma_start(l3[:], offs3)
         nc.sync.dma_start(out=w_w[:].bitcast(I32), in_=w_words[0].rearrange("p n t -> p (n t)").bitcast(I32))
@@ -98,11 +105,12 @@ def tile_list_gatedpage_bank_one_scattered_kernel(
         nc.vector.tensor_copy(out=planes[:, 0 : 2 * R].rearrange("p (w t m) -> p w m t", w=2, t=PACK),
                               in_=ww_s[:].rearrange("p (w m t) -> p w m t", w=2, t=PACK))
         nc.vector.tensor_copy(out=planes[:, 2 * R + J : 2 * R + 2 * J].bitcast(I32), in_=note_s[:].bitcast(I32))
-        for quad in range(1, 4):
-            nc.sync.dma_start(out=planes[32 * quad : 32 * quad + 4, :].bitcast(I32),
-                              in_=planes[4 * quad : 4 * quad + 4, :].bitcast(I32))
+        for quad in range(1, P // QUADRANT):
+            nc.sync.dma_start(out=planes[QUADRANT * quad : QUADRANT * quad + QUAD_ROWS, :].bitcast(I32),
+                              in_=planes[QUAD_ROWS * quad : QUAD_ROWS * (quad + 1), :].bitcast(I32))
+
         nc.vector.tensor_copy(note_w[:], xo_w[:].indirect(l2[:]))
-        for t in range(2, PACK):
+        for t in range(EARLY_TABLES, PACK):
             table.append(keep.tile([P, Q], F32, name="table%d" % t, tag="wide%d" % t))
             nc.sync.dma_start(out=table[t][:], in_=tg_rows[t])
         nc.vector.tensor_copy(tok_w[:], xt_w[:].indirect(l1[:]))
@@ -113,7 +121,7 @@ def tile_list_gatedpage_bank_one_scattered_kernel(
         tok_p = planes[:, 2 * R : 2 * R + J]
         note_p = planes[:, 2 * R + J : 2 * R + 2 * J]
 
-        acc = [psum.tile([P, 512], F32, name="acc%d" % t) for t in range(PACK)]
+        acc = [psum.tile([P, BANK], F32, name="acc%d" % t) for t in range(PACK)]
         for t in range(PACK):
             cols = slice(P * t, P * (t + 1))
             nc.tensor.matmul_mx(out=acc[t][:, 0:J], lhsT=wp_w[:, cols].bitcast(E4M3), lhsT_scale=wp_s[:, cols],
@@ -125,39 +133,40 @@ def tile_list_gatedpage_bank_one_scattered_kernel(
         slots = [sb([P, J], F32, "slots%d" % t) for t in range(PACK)]
         gated = [sb([P, C], F32, "gated%d" % t) for t in range(PACK)]
         hid = sb([P, O, PACK], BF16, "hid")
-        picked = sb([P, PACK, O], BF16, "picked")
 
         def look_up_gate(t):
             nc.scalar.activation(out=gate[t][:], in_=table[t][:].indirect(l4[:]), func=ACT.Sigmoid,
                                  bias=offset[:, t : t + 1], scale=slope[:, t : t + 1])
 
-        for t in range(3):
+        for t in range(EARLY_TABLES):
             look_up_gate(t)
-        for t in (0, 2):
-            nc.vector.tensor_copy(out=slots[t][:], in_=acc[t][:, 0:J])
-            nc.vector.tensor_copy(board[t][:].indirect(l3[:]), slots[t][:])
-        nc.scalar.copy(out=slots[1][:], in_=acc[1][:, 0:J])
-        look_up_gate(3)
-        nc.scalar.copy(out=slots[3][:], in_=acc[3][:, 0:J])
-        for t in (1, 3):
+        for t in range(0, PACK, 2):
+            for u in (t, t + 1):
+                nc.vector.tensor_copy(out=slots[u][:], in_=acc[u][:, 0:J])
             nc.scalar.activation(out=board[t][:].indirect(l3[:]), in_=slots[t][:], func=ACT.Copy)
+            nc.vector.tensor_copy(board[t + 1][:].indirect(l3[:]), slots[t + 1][:])
+            look_up_gate(EARLY_TABLES + t // 2)
+
+        picked = keep.tile([P, PACK, O], BF16, name="picked", tag="picked")
         for t in range(PACK):
             nc.vector.tensor_tensor(gated[t][:], board[t][:], gate[t][:], MULT)
-        for t in range(3):
+        last = PACK - 1
+        for t in range(last):
             nc.scalar.activation(out=picked[:, t, :], in_=gated[t][:].indirect(l5[:]), func=ACT.Copy)
-        nc.vector.tensor_copy(picked[:, 3, :], gated[3][:].indirect(l5[:]))
+        nc.vector.tensor_copy(picked[:, last, :], gated[last][:].indirect(l5[:]))
         nc.vector.tensor_copy(out=hid[:], in_=picked[:].rearrange("p t o -> p o t"))
-        page = [keep.tile([P, E], F32, name="page%d" % h, tag="wide%d" % (h + 2)) for h in range(2)]
-        for h in range(2):
+
+        page = [keep.tile([P, E], F32, name="page%d" % h, tag="wide%d" % (h + EARLY_TABLES)) for h in range(N // P)]
+        for h in range(N // P):
             nc.gpsimd.memset(page[h][:], 0.0)
 
         hid_w = sb([P, O], U32, "hid_w")
         hid_s = sb([P, O], U8, "hid_s")
         nc.vector.quantize_mx(out=hid_w[:].bitcast(E5M2), scales=hid_s[:], in_=hid[:].rearrange("p o t -> p (o t)"))
 
-        res = [psum.tile([P, 512], F32, name="res%d" % h) for h in range(2)]
-        rows = [sb([P, O], F32, "rows%d" % h) for h in range(2)]
-        for h in range(2):
+        res = [psum.tile([P, BANK], F32, name="res%d" % h) for h in range(N // P)]
+        rows = [sb([P, O], F32, "rows%d" % h) for h in range(N // P)]
+        for h in range(N // P):
             cols = slice(P * h, P * (h + 1))
             nc.tensor.matmul_mx(out=res[h][:, 0:O], lhsT=wb_w[:, cols].bitcast(E2M1), lhsT_scale=wb_s[:, cols],
                                 rhs=hid_w[:].bitcast(E5M2), rhs_scale=hid_s[:], start=True, stop=True)

from contextlib import ExitStack

import concourse.mybir as mybir

F32 = mybir.dt.float32
BF16 = mybir.dt.bfloat16
I32 = mybir.dt.int32
U32 = mybir.dt.uint32
U16 = mybir.dt.uint16
U8 = mybir.dt.uint8
E4M3 = mybir.dt.float8_e4m3fn_x4
E5M2 = mybir.dt.float8_e5m2_x4
E2M1 = mybir.dt.float4_e2m1fn_x4
ACT = mybir.ActivationFunctionType
MULT = mybir.AluOpType.mult

P = 128
PACK = 4
K_PASS = P * PACK
SCALE_ROWS = K_PASS // 32
QUADRANT = 32
QUAD_ROWS = 4
BANK = 512
LIST_ROWS = 16
T, Z, J, R, C, Q, O, N, E = 1024, 1024, 256, 512, 512, 1024, 256, 256, 1024
EARLY_TABLES = 2
FLOPS = 2 * K_PASS * R * J * 2 + 2 * R * N * O


def tile_list_gatedpage_bank_one_scattered_kernel(
    tc, xt_words, xt_scales, w_words, w_scales, xo_words, xo_scales, w0_words, w0_scales,
    tg, sg, bg, wb_words, wb_scales, offs, offs2, offs3, offs4, offs5, offs6, out,
):
    nc = tc.nc
    with ExitStack() as ctx:
        keep = ctx.enter_context(tc.tile_pool(name="keep", bufs=1))
        psum = ctx.enter_context(tc.psum_pool(name="psum", bufs=1))

        def sb(shape, dtype, name):
            return keep.tile(shape, dtype, name=name, align_bytes=64)

        l1 = keep.tile([P, J // LIST_ROWS], U16, name="l1")
        l2 = keep.tile([P, J // LIST_ROWS], U16, name="l2")
        l3 = keep.tile([P, J // LIST_ROWS], U16, name="l3")
        l4 = keep.tile([P, C // LIST_ROWS], U16, name="l4")
        l5 = keep.tile([P, O // LIST_ROWS], U16, name="l5")
        l6 = keep.tile([P, O // LIST_ROWS], U16, name="l6")

        xt_w = sb([P, T], U16, "xt_w")
        xt_s = sb([P, T], U8, "xt_s")
        xo_w = keep.tile([P, Z], U32, name="xo_w", tag="wide3")
        xo_s = sb([P, Z], U8, "xo_s")
        w_w = sb([P, R], U32, "w_w")
        w0_w = sb([P, R], U16, "w0_w")
        ww_s = sb([P, 2 * R], U8, "ww_s")
        planes = sb([P, 2 * R + 2 * J + N], U8, "planes")
        wb_s = planes[:, 2 * R + 2 * J : 2 * R + 2 * J + N]
        slope = keep.tile([P, PACK], F32, name="slope", tag="picked")
        offset = sb([P, PACK], F32, "offset")
        table = [keep.tile([P, Q], F32, name="table%d" % t, tag="wide%d" % t) for t in range(EARLY_TABLES)]
        board = [sb([P, C], F32, "board%d" % t) for t in range(PACK)]

        for scale_bytes in (xt_s[:], xo_s[:], ww_s[:], wb_s):
            nc.vector.memset(scale_bytes.bitcast(I32), 0)
        for t in range(PACK):
            nc.vector.memset(board[t][:], 0.0)

        tg_rows = tg.rearrange("(p t) q -> t p q", t=PACK)
        for t in range(EARLY_TABLES):
            nc.gpsimd.dma_start(out=table[t][:], in_=tg_rows[t])
        wb_w = sb([P, N], U16, "wb_w")
        nc.sync.dma_start(l1[:], offs)
        nc.sync.dma_start(l2[:], offs2)
        nc.sync.dma_start(l4[:], offs4)
        nc.sync.dma_start(out=slope[:], in_=sg.rearrange("(p t) o -> p (t o)", t=PACK))
        nc.sync.dma_start(out=offset[:], in_=bg.rearrange("(p t) o -> p (t o)", t=PACK))
        nc.sync.dma_start(out=xt_s[0:SCALE_ROWS, :].bitcast(I32), in_=xt_scales[0].bitcast(I32))
        nc.sync.dma_start(out=xo_s[0:SCALE_ROWS, :].bitcast(I32), in_=xo_scales[0].bitcast(I32))
        nc.sync.dma_start(out=xo_w[:].bitcast(I32), in_=xo_words[0].rearrange("p n t -> p (n t)").bitcast(I32))
        nc.sync.dma_start(out=ww_s[0:SCALE_ROWS, 0:R].bitcast(I32), in_=w_scales[0].bitcast(I32))
        nc.sync.dma_start(out=ww_s[0:SCALE_ROWS, R : 2 * R].bitcast(I32), in_=w0_scales[0].bitcast(I32))
        nc.sync.dma_start(out=wb_s[0:SCALE_ROWS, :].bitcast(I32), in_=wb_scales[0].bitcast(I32))
        nc.sync.dma_start(out=xt_w[:].bitcast(I32), in_=xt_words[0].bitcast(I32))
        nc.sync.dma_start(l3[:], offs3)
        nc.sync.dma_start(out=w_w[:].bitcast(I32), in_=w_words[0].rearrange("p n t -> p (n t)").bitcast(I32))
        nc.sync.dma_start(out=w0_w[:].bitcast(I32), in_=w0_words[0].bitcast(I32))
        nc.sync.dma_start(l5[:], offs5)
        nc.sync.dma_start(l6[:], offs6)
        nc.sync.dma_start(out=wb_w[:].bitcast(I32), in_=wb_words[0].bitcast(I32))

        tok_w = sb([P, J], U16, "tok_w")
        tok_s = sb([P, J], U8, "tok_s")
        note_w = sb([P, J], U32, "note_w")
        note_s = keep.tile([P, J], U8, name="note_s", tag="wide2")
        wp_w = sb([P, R], U32, "wp_w")
        w0p_w = sb([P, R], U16, "w0p_w")

        def deal(dealt, natural):
            nc.vector.tensor_copy(out=dealt[:].rearrange("p (t m) -> p m t", t=PACK),
                                  in_=natural[:].rearrange("p (m t) -> p m t", t=PACK))

        nc.vector.tensor_copy(tok_s[:], xt_s[:].indirect(l1[:]))
        nc.vector.tensor_copy(note_s[:], xo_s[:].indirect(l2[:]))
        nc.vector.tensor_copy(out=planes[:, 2 * R : 2 * R + J].bitcast(I32), in_=tok_s[:].bitcast(I32))
        nc.vector.tensor_copy(out=planes[:, 0 : 2 * R].rearrange("p (w t m) -> p w m t", w=2, t=PACK),
                              in_=ww_s[:].rearrange("p (w m t) -> p w m t", w=2, t=PACK))
        nc.vector.tensor_copy(out=planes[:, 2 * R + J : 2 * R + 2 * J].bitcast(I32), in_=note_s[:].bitcast(I32))
        for quad in range(1, P // QUADRANT):
            nc.sync.dma_start(out=planes[QUADRANT * quad : QUADRANT * quad + QUAD_ROWS, :].bitcast(I32),
                              in_=planes[QUAD_ROWS * quad : QUAD_ROWS * (quad + 1), :].bitcast(I32))

        nc.vector.tensor_copy(note_w[:], xo_w[:].indirect(l2[:]))
        for t in range(EARLY_TABLES, PACK):
            table.append(keep.tile([P, Q], F32, name="table%d" % t, tag="wide%d" % t))
            nc.sync.dma_start(out=table[t][:], in_=tg_rows[t])
        nc.vector.tensor_copy(tok_w[:], xt_w[:].indirect(l1[:]))
        deal(wp_w, w_w)
        deal(w0p_w, w0_w)
        wp_s = planes[:, 0:R]
        w0p_s = planes[:, R : 2 * R]
        tok_p = planes[:, 2 * R : 2 * R + J]
        note_p = planes[:, 2 * R + J : 2 * R + 2 * J]

        acc = [psum.tile([P, BANK], F32, name="acc%d" % t) for t in range(PACK)]
        for t in range(PACK):
            cols = slice(P * t, P * (t + 1))
            nc.tensor.matmul_mx(out=acc[t][:, 0:J], lhsT=wp_w[:, cols].bitcast(E4M3), lhsT_scale=wp_s[:, cols],
                                rhs=tok_w[:].bitcast(E2M1), rhs_scale=tok_p, start=True, stop=False)
            nc.tensor.matmul_mx(out=acc[t][:, 0:J], lhsT=w0p_w[:, cols].bitcast(E2M1), lhsT_scale=w0p_s[:, cols],
                                rhs=note_w[:].bitcast(E4M3), rhs_scale=note_p, start=False, stop=True)

        gate = [sb([P, C], F32, "gate%d" % t) for t in range(PACK)]
        slots = [sb([P, J], F32, "slots%d" % t) for t in range(PACK)]
        gated = [sb([P, C], F32, "gated%d" % t) for t in range(PACK)]
        hid = sb([P, O, PACK], BF16, "hid")

        def look_up_gate(t):
            nc.scalar.activation(out=gate[t][:], in_=table[t][:].indirect(l4[:]), func=ACT.Sigmoid,
                                 bias=offset[:, t : t + 1], scale=slope[:, t : t + 1])

        for t in range(EARLY_TABLES):
            look_up_gate(t)
        for t in range(0, PACK, 2):
            for u in (t, t + 1):
                nc.vector.tensor_copy(out=slots[u][:], in_=acc[u][:, 0:J])
            nc.scalar.activation(out=board[t][:].indirect(l3[:]), in_=slots[t][:], func=ACT.Copy)
            nc.vector.tensor_copy(board[t + 1][:].indirect(l3[:]), slots[t + 1][:])
            look_up_gate(EARLY_TABLES + t // 2)

        picked = keep.tile([P, PACK, O], BF16, name="picked", tag="picked")
        for t in range(PACK):
            nc.vector.tensor_tensor(gated[t][:], board[t][:], gate[t][:], MULT)
        last = PACK - 1
        for t in range(last):
            nc.scalar.activation(out=picked[:, t, :], in_=gated[t][:].indirect(l5[:]), func=ACT.Copy)
        nc.vector.tensor_copy(picked[:, last, :], gated[last][:].indirect(l5[:]))
        nc.vector.tensor_copy(out=hid[:], in_=picked[:].rearrange("p t o -> p o t"))

        page = [keep.tile([P, E], F32, name="page%d" % h, tag="wide%d" % (h + EARLY_TABLES)) for h in range(N // P)]
        for h in range(N // P):
            nc.gpsimd.memset(page[h][:], 0.0)

        hid_w = sb([P, O], U32, "hid_w")
        hid_s = sb([P, O], U8, "hid_s")
        nc.vector.quantize_mx(out=hid_w[:].bitcast(E5M2), scales=hid_s[:], in_=hid[:].rearrange("p o t -> p (o t)"))

        res = [psum.tile([P, BANK], F32, name="res%d" % h) for h in range(N // P)]
        rows = [sb([P, O], F32, "rows%d" % h) for h in range(N // P)]
        for h in range(N // P):
            cols = slice(P * h, P * (h + 1))
            nc.tensor.matmul_mx(out=res[h][:, 0:O], lhsT=wb_w[:, cols].bitcast(E2M1), lhsT_scale=wb_s[:, cols],
                                rhs=hid_w[:].bitcast(E5M2), rhs_scale=hid_s[:], start=True, stop=True)
        nc.scalar.copy(out=rows[0][:], in_=res[0][:, 0:O])
        nc.scalar.activation(out=page[0][:].indirect(l6[:]), in_=rows[0][:], func=ACT.Copy)
        nc.vector.tensor_copy(out=rows[1][:], in_=res[1][:, 0:O])
        nc.vector.tensor_copy(page[1][:].indirect(l6[:]), rows[1][:])
        nc.scalar.dma_start(out=out[0:P, :], in_=page[0][:])
        nc.sync.dma_start(out=out[P : 2 * P, :], in_=page[1][:])
